import numpy as np
import ml_dtypes


def mxq(x, axis, fmt="e4m3"):
    dtype, down = {"e4m3": (ml_dtypes.float8_e4m3fn, 7), "e5m2": (ml_dtypes.float8_e5m2, 14)}[fmt]
    v = np.moveaxis(np.asarray(x, np.float32).astype(ml_dtypes.bfloat16).astype(np.float64), axis, -1)
    blocks = v.reshape(v.shape[:-1] + (-1, 32))
    amax = np.abs(blocks).max(-1, keepdims=True)
    byte = np.maximum(np.where(amax > 0, np.frexp(amax)[1] - 1 + 127, 0) - down, 1)
    scale = np.exp2(byte - 127.0)
    codes = (blocks / scale).astype(np.float32).astype(dtype).astype(np.float64)
    return np.moveaxis((codes * scale).reshape(v.shape), -1, axis)


WIDE = False


def mx_kscale(k):
    if not WIDE:
        return np.ones(k)
    levels = np.array([10, -10, 5, -5, 0])
    if k % 512:
        return np.exp2(np.random.permutation(np.resize(levels, k // 32))).repeat(32)
    a = np.empty((k // 512, 16))
    for p in range(k // 512):
        a[p, :8] = np.random.permutation(np.resize(levels, 8))
        for g in range(8):
            far = levels[np.abs(levels - a[p, g]) >= 10]
            a[p, g + 8] = far[np.random.randint(len(far))]
    return np.exp2(a.ravel()).repeat(32)


BF16 = ml_dtypes.bfloat16


def bf(x):
    return np.asarray(x, np.float32).astype(BF16)


def f64(x):
    return np.asarray(x).astype(np.float64)


E2M1 = np.array([0.0, 0.5, 1.0, 1.5, 2.0, 3.0, 4.0, 6.0, -0.0, -0.5, -1.0, -1.5, -2.0, -3.0, -4.0, -6.0])


def pack_weight(w, fmt):
    k, n = w.shape
    w = f64(bf(w)).reshape(k // 32, 32, n)
    amax = np.abs(w).max(1)
    if fmt == "e4m3":
        byte = np.frexp(amax)[1] - 1 + 127 - 7
    else:
        mant, ex = np.frexp(amax / 6.0)
        byte = np.where(mant > 0.5, ex, ex - 1) + 127
    byte = np.clip(np.where(amax > 0, byte, 1), 1, 254)
    scaled = (w * np.exp2(127.0 - byte)[:, None, :]).reshape(k, n).astype(np.float32)
    by_word = np.ascontiguousarray(scaled.reshape(k // 512, 128, 4, n).transpose(0, 1, 3, 2))
    if fmt == "e4m3":
        words = by_word.astype(ml_dtypes.float8_e4m3fn).view(np.uint8)
    else:
        c = by_word.astype(ml_dtypes.float4_e2m1fn).view(np.uint8) & 0xF
        words = c[..., 0::2] | (c[..., 1::2] << 4)
    return np.ascontiguousarray(words), np.ascontiguousarray(byte.astype(np.uint8).reshape(k // 512, 16, n))


def unpack_weight(words, scales, fmt):
    g, p, n, _ = words.shape
    if fmt == "e4m3":
        vals = np.ascontiguousarray(words).view(ml_dtypes.float8_e4m3fn).astype(np.float64)
    else:
        nib = np.empty((g, p, n, 4), np.uint8)
        nib[..., 0::2] = words & 0xF
        nib[..., 1::2] = words >> 4
        vals = E2M1[nib]
    vals = vals * np.repeat(np.exp2(scales.astype(np.float64) - 127.0), 8, axis=1)[..., None]
    return vals.transpose(0, 1, 3, 2).reshape(g * 512, n)
def pack4(w):
    words, scales = pack_weight(w, "e2m1")
    return words.reshape(words.shape[0], 128, -1), scales


def unpack4(words, scales):
    return unpack_weight(words.reshape(words.shape[0], 128, -1, 2), scales, "e2m1")


def planes(Y):
    n, m = Y.shape
    b = f64(bf(Y)).reshape(n // 32, 32, m)
    amax = np.abs(b).max(1)
    byte = np.clip(np.where(amax > 0, np.frexp(amax)[1] - 1 + 127 - 7, 1), 1, 254)
    codes = (b * np.exp2(127.0 - byte)[:, None, :]).reshape(n, m).astype(np.float32).astype(ml_dtypes.float8_e4m3fn).view(np.uint8)
    words = codes.reshape(n // 512, 128, 4, m).transpose(0, 1, 3, 2)
    return np.ascontiguousarray(words), np.ascontiguousarray(byte.astype(np.uint8).reshape(n // 512, 16, m))


T, D, H, N = 1024, 1024, 4, 32
TWO = 2
C = H * TWO * N
SLOTS = N * N


def setup_inputs():
    s = mx_kscale(D)
    t = mx_kscale(SLOTS)
    x = bf(np.random.standard_normal((T, D)) * s)
    wk_words, wk_scales = pack4(np.random.standard_normal((D, C)) * 1.5 / np.sqrt(D) / s[:, None])
    slot_gain = bf(np.random.standard_normal(SLOTS) * np.sqrt(SLOTS) * t)
    values_words, values_scales = pack4(np.random.standard_normal((SLOTS, D)) * 2.0 / np.sqrt(SLOTS) / t[:, None])
    wg_words, wg_scales = pack4(np.random.standard_normal((D, D)) * 1.5 / np.sqrt(D) / s[:, None])
    return {
        "x": x,
        "wk_words": wk_words,
        "wk_scales": wk_scales,
        "slot_gain": slot_gain,
        "values_words": values_words,
        "values_scales": values_scales,
        "wg_words": wg_words,
        "wg_scales": wg_scales,
    }


def softmax(v):
    e = np.exp(v - v.max(-1, keepdims=True))
    return e / e.sum(-1, keepdims=True)


def product_key_weights(sc):
    p = softmax(sc)
    p1 = p[:, :, 0, :]
    p2 = p[:, :, 1, :]
    w = np.sum(p1[:, :, :, None] * p2[:, :, None, :], axis=1)
    return w.reshape(w.shape[0], SLOTS)


def core(x, wk_words, wk_scales, slot_gain, values_words, values_scales, wg_words, wg_scales):
    xq = mxq(f64(x), 1, "e4m3")
    sc = (xq @ unpack4(wk_words, wk_scales)).reshape(x.shape[0], H, TWO, N)
    w = product_key_weights(sc)
    wg_slots = w * f64(slot_gain)[None, :]
    mem = mxq(wg_slots, 1, "e4m3") @ unpack4(values_words, values_scales)
    a = xq @ unpack4(wg_words, wg_scales)
    gate = a * (1.0 / (1.0 + np.exp(-a)))
    return mem * gate


def reference(x, wk_words, wk_scales, slot_gain, values_words, values_scales, wg_words, wg_scales):
    R_out = core(x, wk_words, wk_scales, slot_gain, values_words, values_scales, wg_words, wg_scales)
    words, scales = planes(R_out.T)
    return R_out, words, scales

from contextlib import ExitStack

import concourse.mybir as mybir
from concourse.masks import make_identity

T, D, H, N = 1024, 1024, 4, 32
SLOTS = N * N
FLOPS = 2 * T * (D * 2 * H * N + SLOTS * D + D * D)

F32 = mybir.dt.float32
BF16 = mybir.dt.bfloat16
I32 = mybir.dt.int32
U32 = mybir.dt.uint32
U8 = mybir.dt.uint8
E4M3 = mybir.dt.float8_e4m3fn_x4
E2M1 = mybir.dt.float4_e2m1fn_x4
ALU = mybir.AluOpType
ACT = mybir.ActivationFunctionType
AXIS = mybir.AxisListType

P = 128
TILES = T // P

ORDER = (
    "D:0 D:1 D:2 D:3 D:4 D:5 XT:0 XC:0 XT:1 XC:1 D:6 XQ:0 SM:0 DT:0 XT:2 XC:2 "
    "XQ:1 MX:0 EX:0 D:7 SM:1 DT:1 XT:3 XQ:2 MX:1 EX:1 XT:4 XC:4 XV:3 SM:2 DT:2 XQ:3 "
    "SW:0 D:8 XT:5 MX:2 EX:2 XQ:4 SM:3 DT:3 XT:6 XC:6 XV:5 SW:1 D:9 MX:3 EX:3 XQ:5 "
    "ZZ:0 SM:4 DT:4 XT:7 XQ:6 MX:4 EX:4 NM:0 SA:0 XV:7 SM:5 DT:5 D:10 SW:2 ZZ:1 XQ:7 "
    "MX:5 EX:5 SV:0 SM:6 DT:6 NM:1 SA:1 D:11 SW:3 ZZ:2 MX:6 EX:6 SM:7 DT:7 SV:1 NM:2 "
    "SA:2 MX:7 EX:7 SW:4 DM:0:0 GV:0:0 ZZ:3 DM:0:1 GV:0:1 DV:0:0 RO:0:0 SV:2 NM:3 SA:3 GA:0:0 SI:0:0 "
    "SW:5 DM:1:0 GV:1:0 ZZ:4 DM:1:1 GV:1:1 DV:1:0 RO:1:0 SV:3 NM:4 SA:4 GA:0:1 SI:0:1 DV:0:1 RO:0:1 SW:6 "
    "DM:2:0 GV:2:0 ZZ:5 GA:1:0 SI:1:0 DM:2:1 GV:2:1 DV:2:0 RO:2:0 SV:4 NM:5 SA:5 DV:1:1 RO:1:1 SW:7 DM:3:0 "
    "GV:3:0 ZZ:6 GA:1:1 SI:1:1 DM:3:1 GV:3:1 DV:3:0 RO:3:0 SV:5 GA:2:0 SI:2:0 NM:6 SA:6 DV:2:1 RO:2:1 DM:4:0 "
    "GV:4:0 ZZ:7 DM:4:1 GV:4:1 DV:4:0 RO:4:0 SV:6 GA:2:1 SI:2:1 NM:7 SA:7 DV:3:1 RO:3:1 GA:3:0 SI:3:0 DM:5:0 "
    "GV:5:0 DM:5:1 GV:5:1 DV:5:0 RO:5:0 SV:7 UT:0 UC:0 DV:4:1 RO:4:1 UT:1 UC:1 GA:3:1 SI:3:1 DM:6:0 GV:6:0 "
    "DM:6:1 GV:6:1 GA:4:0 SI:4:0 DV:6:0 RO:6:0 UQ:0 DV:5:1 RO:5:1 DM:7:0 GV:7:0 DM:7:1 GV:7:1 UQ:1 GA:4:1 SI:4:1 "
    "MM:0:0 PR:0:0 YR:0 DV:7:0 RO:7:0 UT:2 UC:2 UT:3 UC:3 MM:0:1 PR:0:1 GA:5:0 SI:5:0 DV:6:1 RO:6:1 UQ:2 "
    "MM:1:0 PR:1:0 YR:1 YS:0 MM:1:1 PR:1:1 GA:5:1 SI:5:1 DV:7:1 RO:7:1 UQ:3 MM:2:0 PR:2:0 YR:2 GA:6:0 SI:6:0 "
    "UT:4 UC:4 UT:5 UC:5 YS:1 MM:2:1 PR:2:1 UQ:4 MM:3:0 PR:3:0 YR:3 YS:2 GA:6:1 SI:6:1 MM:3:1 PR:3:1 "
    "GA:7:0 SI:7:0 UQ:5 MM:4:0 PR:4:0 YR:4 YT:0 YC:0 YT:1 YC:1 UT:6 UC:6 UT:7 UC:7 YS:3 MM:4:1 "
    "PR:4:1 YQ:0 UQ:6 MM:5:0 PR:5:0 YR:5 GA:7:1 SI:7:1 YS:4 MM:5:1 PR:5:1 YQ:1 UQ:7 MM:6:0 PR:6:0 YR:6 "
    "YT:2 YC:2 YT:3 YC:3 YS:5 MM:6:1 PR:6:1 YQ:2 MM:7:0 PR:7:0 YR:7 YS:6 MM:7:1 PR:7:1 YQ:3 YT:4 "
    "YC:4 YT:5 YC:5 YS:7 YQ:4 YQ:5 YT:6 YC:6 YT:7 YC:7 YQ:6 YQ:7 "
)


def tile_productkeysoftmemoryplus_x2_kernel(
    tc, x, wk_words, wk_scales, slot_gain, values_words, values_scales, wg_words, wg_scales, out_0, out_1, out_2
):
    nc = tc.nc
    with ExitStack() as ctx:
        keep = ctx.enter_context(tc.tile_pool(name="keep", bufs=1))
        work = ctx.enter_context(tc.tile_pool(name="work", bufs=2))
        psum = ctx.enter_context(tc.psum_pool(name="psum", bufs=2))
        ctx.enter_context(tc.manual_schedule())

        def kept(name, shape, dtype):
            t = keep.tile(shape, dtype, name=name, align_bytes=64)
            return t

        def worked(name, shape, dtype, bufs):
            t = work.tile(shape, dtype, name=name, tag=name, bufs=bufs, align_bytes=64)
            return t

        def bank(tag, shape, bufs):
            t = psum.tile(shape, F32, name=tag, tag=tag, bufs=bufs)
            return t

        zeros = kept("zeros", [P, 512], BF16)
        nc.vector.memset(zeros[:], 0.0)
        ident = kept("ident", [P, P], F32)
        make_identity(nc, ident[:])

        wk_plane = kept("wk_plane", [P, 2, 256], U8)
        nc.vector.memset(wk_plane[:].rearrange("p g n -> p (g n)").bitcast(I32), 0)
        wg_plane = kept("wg_plane", [P, 2, D], U8)
        nc.vector.memset(wg_plane[:].rearrange("p g n -> p (g n)").bitcast(I32), 0)
        va_plane = kept("va_plane", [P, 2, D], U8)
        nc.vector.memset(va_plane[:].rearrange("p g n -> p (g n)").bitcast(I32), 0)

        x_raw = []
        for i in range(TILES):
            x_raw.append(kept("x_raw%d" % i, [P, D], BF16))

        def load_x(i):
            nc.sync.dma_start(out=x_raw[i][:], in_=x[P * i : P * (i + 1), :])

        def load_words(dst, src):
            nc.sync.dma_start(out=dst[:].bitcast(I32), in_=src.rearrange("g p b -> p g b").bitcast(I32))

        def load_scales(dst, src):
            for q in range(4):
                nc.sync.dma_start(
                    out=dst[32 * q : 32 * q + 4, :, :].bitcast(I32),
                    in_=src[:, 4 * q : 4 * q + 4, :].rearrange("g r n -> r g n").bitcast(I32),
                )

        wk_raw = kept("wk_raw", [P, 2, 512], U8)
        wg_w = kept("wg_w", [P, 2, 2 * D], U8)
        va_w = kept("va_w", [P, 2, 2 * D], U8)
        gain_raw = kept("gain_raw", [P, N], BF16)

        load_x(0)
        load_words(wk_raw, wk_words)
        load_x(1)
        load_scales(wk_plane, wk_scales)
        load_x(2)
        load_words(wg_w, wg_words)
        load_scales(wg_plane, wg_scales)
        for i in range(3, TILES):
            load_x(i)
        for a in range(4):
            nc.sync.dma_start(out=gain_raw[32 * a : 32 * (a + 1), :], in_=slot_gain.rearrange("(i j) -> i j", j=N))
        load_words(va_w, values_words)
        load_scales(va_plane, values_scales)

        mask_a = kept("mask_a", [P, 4], F32)
        nc.vector.tensor_reduce(out=mask_a[:], in_=ident[:].rearrange("p (x a) -> p a x", a=4), axis=AXIS.X, op=ALU.add)
        mask_b = kept("mask_b", [P, 8], F32)
        nc.vector.tensor_reduce(
            out=mask_b[:], in_=ident[:].rearrange("p (h b a) -> p b h a", h=4, b=8), axis=AXIS.XY, op=ALU.add
        )

        wk_w = kept("wk_w", [P, 2, 2, 256], U8)
        wk_s = kept("wk_s", [P, 2, 2, 128], U8)
        gain = kept("gain", [P, 8, 16, 4], F32)

        def prepare_wk():
            for g in range(2):
                nc.vector.tensor_copy(
                    out=wk_w[:, g, :, :].rearrange("p f b -> p (f b)").bitcast(I32).rearrange("p (f h k) -> p f h k", f=2, h=4),
                    in_=wk_raw[:, g, :].bitcast(I32).rearrange("p (h f k) -> p f h k", f=2, h=4),
                )
                nc.vector.tensor_copy(
                    out=wk_s[:, g, :, :].rearrange("p f b -> p (f b)").bitcast(I32).rearrange("p (f h k) -> p f h k", f=2, h=4),
                    in_=wk_plane[:, g, :].bitcast(I32).rearrange("p (h f k) -> p f h k", f=2, h=4),
                )

        def prepare_gain():
            nc.vector.tensor_copy(
                out=gain[:],
                in_=gain_raw[:].rearrange("p (j o l) -> p j o l", j=8, o=1).to_broadcast([P, 8, 16, 4]),
            )

        y_plane = kept("y_plane", [P, 2, T], U8)
        st = {}

        def x_turn(i):
            tr = bank("tr", [P, 4, P], 2)
            words = x_raw[i][:].bitcast(F32)
            for g in range(2):
                for u in range(2):
                    nc.tensor.transpose(tr[:, 2 * g + u, :], words[:, 256 * g + u : 256 * (g + 1) : 2], ident[:])
            st["xt", i] = tr

        def words_out(name, tr, copy):
            grouped = worked(name, [P, D], BF16, 4)
            copy(
                out=grouped[:].bitcast(F32).rearrange("p (g r u) -> p g r u", g=2, u=2),
                in_=tr[:].rearrange("p (g u) r -> p g r u", g=2),
            )
            return grouped

        def x_copy(i):
            st["xg", i] = words_out("xg", st["xt", i], nc.scalar.copy)

        def x_quant(i):
            codes = kept("x_codes%d" % i, [P, 256], U32)
            scales = kept("x_scales%d" % i, [P, 256], U8)
            nc.vector.quantize_mx(out=codes[:].bitcast(E4M3), scales=scales[:], in_=st["xg", i][:])
            st["x", i] = (codes, scales)

        def s_mul(i):
            codes, scales = st["x", i]
            sp = bank("sw", [P, 2, P], 2)
            for f in range(2):
                for g in range(2):
                    cols = slice(P * g, P * (g + 1))
                    nc.tensor.matmul_mx(
                        out=sp[:, f, :],
                        lhsT=wk_w[:, g, f, :].bitcast(E2M1),
                        lhsT_scale=wk_s[:, g, f, :],
                        rhs=codes[:, cols].bitcast(E4M3),
                        rhs_scale=scales[:, cols],
                        start=(g == 0),
                        stop=(g == 1),
                    )
            st["sp", i] = sp

        def s_turn(i):
            sc = worked("sc", [P, 2, P], F32, 4)
            for f in range(2):
                nc.vector.transpose(out=sc[:, f, :], in_=st["sp", i][:, f, :])
            st["sc", i] = sc

        def s_max(i):
            mx = worked("mx", [P, 8], F32, 4)
            nc.vector.tensor_reduce(
                out=mx[:],
                in_=st["sc", i][:].rearrange("p f (g k) -> p (f g) k", k=N),
                axis=AXIS.X,
                op=ALU.max,
                negate=True,
            )
            st["mx", i] = mx

        def s_exp(i):
            ex = worked("ex", [P, 8, N], F32, 8)
            zs = worked("zs", [P, 8], F32, 8)
            for y in range(8):
                nc.scalar.activation(
                    out=ex[:, y, :],
                    in_=st["sc", i][:].rearrange("p f (g k) -> p (f g) k", k=N)[:, y, :],
                    func=ACT.Exp,
                    bias=st["mx", i][:, y : y + 1],
                    accum_out=zs[:, y : y + 1],
                )
            st["ex", i] = (ex, zs)

        def s_norm(i):
            zs = st["ex", i][1]
            zz = worked("zz", [P, 4], F32, 5)
            nc.vector.tensor_tensor(out=zz[:], in0=zs[:, 0:4], in1=zs[:, 4:8], op=ALU.mult)
            rz = worked("rz", [P, 4], F32, 5)
            nc.vector.reciprocal(out=rz[:], in_=zz[:])
            st["rz", i] = rz

        def p_norm(i):
            p1 = worked("p1", [P, 4, N], F32, 4)
            nc.vector.tensor_tensor(
                out=p1[:],
                in0=st["ex", i][0][:, 0:4, :],
                in1=st["rz", i][:].unsqueeze(2).to_broadcast([P, 4, N]),
                op=ALU.mult,
            )
            st["p1", i] = p1

        def spread_a(i):
            s1 = worked("s1", [P, 4, 4, N], F32, 6)
            for a in range(4):
                nc.scalar.activation(
                    out=s1[:, :, a, :], in_=st["p1", i][:], func=ACT.Copy, scale=mask_a[:, a : a + 1]
                )
            st["s1", i] = s1

        def w_mul(i, q):
            wp = bank("sw", [P, 2, 256], 2)
            for r in range(2):
                g = 2 * q + r
                nc.tensor.matmul(
                    wp[:, r, :],
                    lhsT=st["s1", i][:, g, :, :].rearrange("p a k -> p (a k)"),
                    rhs=st["s2", i][:, g, :, :].rearrange("p b k -> p (b k)"),
                    start=True,
                    stop=True,
                )
            st["wp", i, q] = wp

        def w_gain(i, q):
            ub = worked("ub", [P, 8, 16, 4], BF16, 4)
            nc.vector.tensor_tensor(
                out=ub[:],
                in0=st["wp", i, q][:].rearrange("p r (b j l) -> p j (r b) l", b=8, j=8),
                in1=gain[:],
                op=ALU.mult,
            )
            st["ub", i, q] = ub

        def w_turn(i, q):
            ut = worked("ut", [P, 512], BF16, 8)
            nc.vector.transpose(
                out=ut[:].bitcast(F32), in_=st["ub", i, q][:].rearrange("p j x l -> p (j x l)").bitcast(F32)
            )
            st["ut", i, q] = ut

        def w_order(i, q):
            ur = kept("ur%d_%d" % (i, q), [P, 512], BF16)
            nc.scalar.copy(
                out=ur[:].bitcast(F32).rearrange("p (i h l) -> p h i l", h=2, l=4),
                in_=st["ut", i, q][:].bitcast(F32).rearrange("p (h l i) -> p h i l", h=2, l=4),
            )
            st["ur", i, q] = ur

        def u_turn(i):
            tr = bank("tr", [P, 2, 2, P], 2)
            for q in range(2):
                words = st["ur", i, q][:].bitcast(F32)
                for g in range(2):
                    nc.tensor.transpose(tr[:, g, q, :], words[:, P * g : P * (g + 1)], ident[:])
            st["ut", i] = tr

        def u_copy(i):
            ug = worked("ug", [P, D], BF16, 4)
            nc.scalar.copy(
                out=ug[:].bitcast(F32).rearrange("p (y x a l) -> p y x a l", y=4, x=16, a=4),
                in_=st["ut", i][:].rearrange("p g q (a x l) -> p (g q) x a l", a=4, x=16),
            )
            st["ug", i] = ug

        def u_quant(i):
            codes = worked("u_codes", [P, 256], U32, 5)
            scales = worked("u_scales", [P, 256], U8, 5)
            nc.vector.quantize_mx(out=codes[:].bitcast(E4M3), scales=scales[:], in_=st["ug", i][:])
            st["u", i] = (codes, scales)

        def mx_product(operand, words, plane, n):
            codes, scales = operand
            acc = bank("mm", [P, 512], 4)
            for g in range(2):
                cols = slice(P * g, P * (g + 1))
                nc.tensor.matmul_mx(
                    out=acc[:],
                    lhsT=codes[:, cols].bitcast(E4M3),
                    lhsT_scale=scales[:, cols],
                    rhs=words[:, g, 1024 * n : 1024 * (n + 1)].bitcast(E2M1),
                    rhs_scale=plane[:, g, 512 * n : 512 * (n + 1)],
                    start=(g == 0),
                    stop=(g == 1),
                )
            return acc

        def g_mul(i, n):
            st["ga", i, n] = mx_product(st["x", i], wg_w, wg_plane, n)

        def g_silu(i, n):
            gt = kept("gate%d_%d" % (i, n), [P, 512], F32)
            nc.scalar.activation(out=gt[:], in_=st["ga", i, n][:], func=ACT.Silu)
            st["gt", i, n] = gt

        def m_mul(i, n):
            st["ma", i, n] = mx_product(st["u", i], va_w, va_plane, n)

        def m_gate(i, n):
            res = worked("res", [P, 512], F32, 10)
            nc.vector.tensor_tensor(out=res[:], in0=st["ma", i, n][:], in1=st["gt", i, n][:], op=ALU.mult)
            nc.sync.dma_start(out=out_0[P * i : P * (i + 1), 512 * n : 512 * (n + 1)], in_=res[:])
            st["res", i, n] = res

        def y_round(i, n):
            yb = worked("yb", [P, 2, P, 2], BF16, 12)
            nc.gpsimd.tensor_scalar(
                out=yb[:],
                in0=st["res", i, n][:].rearrange("p (m u e) -> p u m e", u=2, e=2),
                scalar1=1.0,
                scalar2=1.0,
                op0=ALU.mult,
                op1=ALU.mult,
            )
            st["yb", i, n] = yb

        def y_turn(i):
            tr = bank("sw", [P, 4, P], 2)
            for g in range(2):
                words = st["yb", i, g][:].rearrange("p u m e -> p (u m e)").bitcast(F32)
                for u in range(2):
                    nc.tensor.transpose(tr[:, 2 * g + u, :], words[:, P * u : P * (u + 1)], ident[:])
            st["yt", i] = tr

        def y_copy(i):
            st["yg", i] = words_out("yg", st["yt", i], nc.scalar.copy)

        def y_quant(i):
            codes = worked("y_codes", [P, 2, P], U32, 4)
            for g in range(2):
                nc.vector.quantize_mx(
                    out=codes[:, g, :].bitcast(E4M3),
                    scales=y_plane[:, g, P * i : P * (i + 1)],
                    in_=st["yg", i][:, 512 * g : 512 * (g + 1)],
                )
            nc.sync.dma_start(
                out=out_1[:, :, P * i : P * (i + 1), :].rearrange("g p m t -> p g (m t)").bitcast(I32),
                in_=codes[:].bitcast(I32),
            )

        def warm(j):
            acc = bank("mm", [P, 512], 4)
            nc.tensor.matmul(acc[:], lhsT=zeros[:, 0:P], rhs=zeros[:], start=True, stop=True)

        def x_copy_v(i):
            st["xg", i] = words_out("xg", st["xt", i], nc.vector.tensor_copy)

        def spread_half(i, lo, hi, scaled):
            if ("s2", i) not in st:
                st["s2", i] = worked("s2", [P, 4, 8, N], F32, 5)
            for b in range(lo, hi):
                scaled(st["s2", i][:, :, b, :], st["ex", i][0][:, 4:8, :], mask_b[:, b : b + 1])

        def scaled_v(out, in_, mask):
            nc.vector.tensor_scalar(out=out, in0=in_, scalar1=mask, scalar2=None, op0=ALU.mult)

        def scaled_s(out, in_, mask):
            nc.scalar.activation(out=out, in_=in_, func=ACT.Copy, scale=mask)

        def spread_bv(i):
            spread_half(i, 0, 4, scaled_v)

        def spread_bs(i):
            spread_half(i, 4, 8, scaled_s)

        def y_round_g(i):
            y_round(i, 0)

        def y_round_s(i):
            yb = worked("yb", [P, 2, P, 2], BF16, 12)
            nc.scalar.copy(out=yb[:], in_=st["res", i, 1][:].rearrange("p (m u e) -> p u m e", u=2, e=2))
            st["yb", i, 1] = yb

        units = {
            "XT": x_turn, "XC": x_copy, "XQ": x_quant, "SM": s_mul, "DT": s_turn, "MX": s_max, "EX": s_exp,
            "ZZ": s_norm, "NM": p_norm, "SA": spread_a, "SV": spread_bv, "SW": spread_bs, "XV": x_copy_v, "D": warm, "DM": w_mul, "GV": w_gain, "DV": w_turn,
            "RO": w_order, "UT": u_turn, "UC": u_copy, "UQ": u_quant, "GA": g_mul, "SI": g_silu, "MM": m_mul,
            "PR": m_gate, "YR": y_round_g, "YS": y_round_s, "YT": y_turn, "YC": y_copy, "YQ": y_quant,
        }
        prepare_wk()
        prepared = []
        for token in ORDER.split():
            parts = token.split(":")
            if parts[0] == "GV" and not prepared:
                prepare_gain()
                prepared.append(1)
            units[parts[0]](*[int(v) for v in parts[1:]])
        for q in range(4):
            nc.sync.dma_start(
                out=out_2[:, 4 * q : 4 * q + 4, :].rearrange("g r n -> r g n").bitcast(I32),
                in_=y_plane[32 * q : 32 * q + 4, :, :].bitcast(I32),
            )
